import numpy as np
import ml_dtypes


def mxq(x, axis, fmt="e4m3"):
    dtype, down = {"e4m3": (ml_dtypes.float8_e4m3fn, 7), "e5m2": (ml_dtypes.float8_e5m2, 14)}[fmt]
    v = np.moveaxis(np.asarray(x, np.float32).astype(ml_dtypes.bfloat16).astype(np.float64), axis, -1)
    blocks = v.reshape(v.shape[:-1] + (-1, 32))
    amax = np.abs(blocks).max(-1, keepdims=True)
    byte = np.maximum(np.where(amax > 0, np.frexp(amax)[1] - 1 + 127, 0) - down, 1)
    scale = np.exp2(byte - 127.0)
    codes = (blocks / scale).astype(np.float32).astype(dtype).astype(np.float64)
    return np.moveaxis((codes * scale).reshape(v.shape), -1, axis)


WIDE = False


def mx_kscale(k):
    if not WIDE:
        return np.ones(k)
    levels = np.array([10, -10, 5, -5, 0])
    if k % 512:
        return np.exp2(np.random.permutation(np.resize(levels, k // 32))).repeat(32)
    a = np.empty((k // 512, 16))
    for p in range(k // 512):
        a[p, :8] = np.random.permutation(np.resize(levels, 8))
        for g in range(8):
            far = levels[np.abs(levels - a[p, g]) >= 10]
            a[p, g + 8] = far[np.random.randint(len(far))]
    return np.exp2(a.ravel()).repeat(32)


def f64(x):
    return np.asarray(x).astype(np.float64)


def striped(idx):
    return np.tile(idx.reshape(-1, 16).T, (8, 1)).astype(np.uint16)


def unstriped(offs):
    return offs[:16].T.reshape(-1).astype(np.int64)


E2M1 = np.array([0.0, 0.5, 1.0, 1.5, 2.0, 3.0, 4.0, 6.0, -0.0, -0.5, -1.0, -1.5, -2.0, -3.0, -4.0, -6.0])


def pack_weight(w, fmt):
    k, n = w.shape
    w = f64(np.asarray(w, np.float32).astype(ml_dtypes.bfloat16)).reshape(k // 32, 32, n)
    amax = np.abs(w).max(1)
    if fmt == "e4m3":
        byte = np.frexp(amax)[1] - 1 + 127 - 7
    else:
        mant, ex = np.frexp(amax / 6.0)
        byte = np.where(mant > 0.5, ex, ex - 1) + 127
    byte = np.clip(np.where(amax > 0, byte, 1), 1, 254)
    scaled = (w * np.exp2(127.0 - byte)[:, None, :]).reshape(k, n).astype(np.float32)
    by_word = np.ascontiguousarray(scaled.reshape(k // 512, 128, 4, n).transpose(0, 1, 3, 2))
    if fmt == "e4m3":
        words = by_word.astype(ml_dtypes.float8_e4m3fn).view(np.uint8)
    else:
        c = by_word.astype(ml_dtypes.float4_e2m1fn).view(np.uint8) & 0xF
        words = (c[..., 0::2] | (c[..., 1::2] << 4)).reshape(k // 512, 128, 2 * n)
    return np.ascontiguousarray(words), np.ascontiguousarray(byte.astype(np.uint8).reshape(k // 512, 16, n))


def unpack_weight(words, scales, fmt):
    g, _, n = scales.shape
    words = np.ascontiguousarray(words).reshape(g, 128, n, -1)
    if fmt == "e4m3":
        vals = words.view(ml_dtypes.float8_e4m3fn).astype(np.float64)
    else:
        nib = np.empty((g, 128, n, 4), np.uint8)
        nib[..., 0::2] = words & 0xF
        nib[..., 1::2] = words >> 4
        vals = E2M1[nib]
    vals = vals * np.repeat(np.exp2(scales.astype(np.float64) - 127.0), 8, axis=1)[..., None]
    return vals.transpose(0, 1, 3, 2).reshape(g * 512, n)


def sigmoid(v):
    return 1.0 / (1.0 + np.exp(-np.maximum(v, -700.0)))


def d_sigmoid(v):
    s = 1.0 / (1.0 + np.exp(-np.maximum(v, -700.0)))
    return s * (1.0 - s)


K, T, E, C, H, N = 384, 512, 4, 256, 1024, 512


def by_expert(wq, xq):
    return np.concatenate([wq[e].T @ xq[:, e * C:(e + 1) * C] for e in range(E)], axis=1)


def setup_inputs():
    n = np.random.standard_normal
    s = mx_kscale(N)[:, None]
    u = mx_kscale(H)
    first = np.random.permutation(np.repeat(np.arange(E), T // E))
    second = (first + 1 + np.random.permutation(np.repeat(np.arange(E - 1), -(-T // (E - 1)))[:T])) % E
    while np.bincount(second, minlength=E).max() != T // E:
        load = np.bincount(second, minlength=E); hi, lo = int(load.argmax()), int(load.argmin())
        t = np.flatnonzero((second == hi) & (first != lo))[0]; second[t] = lo
    slot_token = np.empty(E * C, np.int64); pos = np.empty((2, T), np.int64); fill = np.zeros(E, np.int64)
    place = np.stack([np.random.permutation(C) for _ in range(E)])
    for r, deal in enumerate((first, second)):
        for t in np.random.permutation(T):
            e = deal[t]; j = e * C + place[e, fill[e]]; fill[e] += 1; slot_token[j] = t; pos[r, t] = j
    g = np.random.uniform(0.2, 0.8, T)
    w_slot = np.empty(E * C); w_slot[pos[0]] = g; w_slot[pos[1]] = 1.0 - g
    w2 = [pack_weight(m, "e2m1") for m in n((E, N, H)) / np.sqrt(N) / s[None] * u[None, None, :]]
    w1 = [pack_weight(m, "e2m1") for m in n((E, H, K)) / np.sqrt(H) / u[None, :, None]]
    w3 = [pack_weight(m, "e2m1") for m in n((E, H, K)) / np.sqrt(H) / u[None, :, None]]
    return {
        "dyT": (n((N, T)) * s).astype(np.float32),
        "a1": n((H, E * C)).astype(np.float32),
        "a3": n((H, E * C)).astype(np.float32),
        "w2_words": np.stack([m[0] for m in w2]),
        "w2_scales": np.stack([m[1] for m in w2]),
        "w1_words": np.stack([m[0] for m in w1]),
        "w1_scales": np.stack([m[1] for m in w1]),
        "w3_words": np.stack([m[0] for m in w3]),
        "w3_scales": np.stack([m[1] for m in w3]),
        "gate": np.tile(w_slot, (N, 1)).astype(np.float32),
        "offs": striped(slot_token),
        "pos1": striped(pos[0]),
        "pos2": striped(pos[1]),
    }


def reference(dyT, a1, a3, w2_words, w2_scales, w1_words, w1_scales, w3_words, w3_scales, gate, offs, pos1, pos2):
    idx = unstriped(offs)
    w2 = np.stack([unpack_weight(w2_words[e], w2_scales[e], "e2m1") for e in range(E)])
    w1 = np.stack([unpack_weight(w1_words[e], w1_scales[e], "e2m1") for e in range(E)])
    w3 = np.stack([unpack_weight(w3_words[e], w3_scales[e], "e2m1") for e in range(E)])
    gq = mxq(f64(gate) * f64(dyT)[:, idx], 0, "e4m3")
    dh = by_expert(w2, gq)
    da1 = dh * f64(a3) * d_sigmoid(f64(a1))
    da3 = dh * sigmoid(f64(a1))
    dx = by_expert(w1, mxq(da1, 0, "e4m3")) + by_expert(w3, mxq(da3, 0, "e4m3"))
    return dx[:, unstriped(pos1)] + dx[:, unstriped(pos2)]

@@ -1,0 +1,310 @@
+from contextlib import ExitStack
+
+import concourse.mybir as mybir
+
+N, T, H, K, E, C = 512, 512, 1024, 384, 4, 256
+P = 128
+PACK = 4
+HH = 2
+B = 2
+KM = K // P
+ON0, ON1 = 0, 0
+
+F32 = mybir.dt.float32
+BF16 = mybir.dt.bfloat16
+U32 = mybir.dt.uint32
+I32 = mybir.dt.int32
+U16 = mybir.dt.uint16
+U8 = mybir.dt.uint8
+FP8X4 = mybir.dt.float8_e4m3fn_x4
+FP4X4 = mybir.dt.float4_e2m1fn_x4
+ACT = mybir.ActivationFunctionType
+ALU = mybir.AluOpType
+
+FLOPS = 2 * E * C * H * (N + 2 * K)
+BYTES = (N * T + 2 * H * E * C + E * C + K * T) * 4 + E * (N + 2 * K) * H // 2 + E * (N + 2 * K) * H // 32 + 2 * 2 * P * (E * C // 16)
+
+
+def tile_moe_bdx_glu_sigmoid_kernel(
+    tc, dyT, a1, a3, w2_words, w2_scales, w1_words, w1_scales, w3_words, w3_scales, gate, offs, pos1, pos2, out
+):
+    nc = tc.nc
+    with ExitStack() as ctx:
+        keep = ctx.enter_context(tc.tile_pool(name="keep", bufs=1))
+        ring2 = ctx.enter_context(tc.tile_pool(name="ring2", bufs=2))
+        ring3 = ctx.enter_context(tc.tile_pool(name="ring3", bufs=3))
+        ring7 = ctx.enter_context(tc.tile_pool(name="ring7", bufs=7))
+        ps1 = ctx.enter_context(tc.psum_pool(name="ps1", bufs=6))
+        ps2 = ctx.enter_context(tc.psum_pool(name="ps2", bufs=2))
+
+        offs_t = keep.tile([P, E * C // 16], U16, name="offs_t")
+        pos1_t = keep.tile([P, T // 16], U16, name="pos1_t")
+        pos2_t = keep.tile([P, T // 16], U16, name="pos2_t")
+        w2_raw = [ring2.tile([P, 2 * H], U8, name="w2_raw", align_bytes=64) for e in range(E)]
+        w2_perm = keep.tile([P, E, 2 * H], U8, name="w2_perm", align_bytes=64)
+        w2s_raw = keep.tile([P, E, H], U8, name="w2s_raw", align_bytes=64)
+        w2s = keep.tile([P, E, H], U8, name="w2s", align_bytes=64)
+        w13 = [keep.tile([P, E, HH, 2 * K], U8, name=f"w13_{j}", align_bytes=64) for j in range(2)]
+        w13s = [keep.tile([P, E, HH, K], U8, name=f"w13s_{j}", align_bytes=64) for j in range(2)]
+        dy = [keep.tile([P, T], F32, name=f"dy_{t}", align_bytes=64) for t in range(PACK)]
+        gate_t = keep.tile([P, E * C], F32, name="gate_t", align_bytes=64)
+        a1_t = [[keep.tile([P, PACK, C], F32, name=f"a1_{e}_{h}", align_bytes=64) for h in range(HH)] for e in range(E)]
+        a3_t = [[keep.tile([P, PACK, C], F32, name=f"a3_{e}_{h}", align_bytes=64) for h in range(HH)] for e in range(E)]
+        dxs = keep.tile([P, KM, E * C], F32, name="dxs", align_bytes=64)
+
+        nc.vector.memset(w2s_raw[:].rearrange("p e i -> p (e i)").bitcast(I32), 0)
+        for j in range(2):
+            nc.gpsimd.memset(w13s[j][:].rearrange("p e s k -> p (e s k)").bitcast(I32), 0)
+
+        a1_v = a1.rearrange("(h q r) c -> h q r c", h=HH, r=PACK)
+        a3_v = a3.rearrange("(h q r) c -> h q r c", h=HH, r=PACK)
+        dy_v = dyT.rearrange("(q t) c -> q t c", t=PACK)
+
+        def load_w2(e):
+            nc.sync.dma_start(w2_raw[e][:].bitcast(I32), w2_words[e, 0].bitcast(I32))
+
+        def load_a(e, h, which):
+            tiles, view = (a1_t, a1_v) if which == 1 else (a3_t, a3_v)
+            nc.sync.dma_start(tiles[e][h][:], view[h][:, :, e * C : (e + 1) * C])
+
+        def load_gate(lo, hi):
+            nc.sync.dma_start(gate_t[:, lo * C : hi * C], gate[0:P, lo * C : hi * C])
+
+        def load_w13(j):
+            words, scales = ((w3_words, w3_scales), (w1_words, w1_scales))[j]
+            for q in range(4):
+                nc.sync.dma_start(
+                    w13s[j][32 * q : 32 * q + 4, :, :, :].rearrange("p e s k -> p (e s) k").bitcast(I32),
+                    scales[:, :, 4 * q : 4 * q + 4, :].rearrange("e s f k -> f (e s) k").bitcast(I32),
+                )
+            nc.sync.dma_start(
+                w13[j][:].rearrange("p e s k -> p (e s) k").bitcast(I32),
+                words.rearrange("e s p k -> p (e s) k").bitcast(I32),
+            )
+
+        def load_w2s():
+            for q in range(4):
+                nc.sync.dma_start(
+                    w2s_raw[32 * q : 32 * q + 4, :, :].bitcast(I32),
+                    w2_scales[:, 0, 4 * q : 4 * q + 4, :].rearrange("e f i -> f e i").bitcast(I32),
+                )
+
+        nc.sync.dma_start(offs_t[:], offs)
+        load_w2(0)
+        load_gate(0, 1)
+        for t in range(PACK):
+            nc.sync.dma_start(dy[t][:], dy_v[:, t, :])
+        load_a(0, 0, 1)
+        load_gate(1, 2)
+        load_w2s()
+        load_a(0, 1, 1)
+        load_w2(1)
+        load_a(0, 0, 3)
+        load_a(0, 1, 3)
+        load_gate(2, E)
+        load_a(1, 0, 1)
+        load_a(1, 1, 1)
+        load_w13(0)
+        load_w13(1)
+        load_a(1, 0, 3)
+        load_a(1, 1, 3)
+        load_w2(2)
+        for h in range(HH):
+            load_a(2, h, 1)
+        for h in range(HH):
+            load_a(2, h, 3)
+        load_w2(3)
+        for which in (1, 3):
+            for h in range(HH):
+                load_a(3, h, which)
+        nc.sync.dma_start(pos1_t[:], pos1)
+        nc.sync.dma_start(pos2_t[:], pos2)
+
+        def permute_words(e):
+            nc.vector.tensor_copy(
+                w2_perm[:, e, :].bitcast(U16).rearrange("p (h r q) -> p h r q", h=HH, r=PACK),
+                w2_raw[e][:].bitcast(U16).rearrange("p (h q r) -> p h r q", h=HH, r=PACK),
+            )
+
+        def permute_scales(e):
+            nc.vector.tensor_copy(
+                w2s[:, e, :].rearrange("p (h r q) -> p h r q", h=HH, r=PACK),
+                w2s_raw[:, e, :].rearrange("p (h q r) -> p h r q", h=HH, r=PACK),
+            )
+
+        gf, gb, gq, gs, sw, banks, dt = {}, {}, {}, {}, {}, {}, {}
+
+        def gather(e, t):
+            if t == 0:
+                gf[e] = ring2.tile([P, PACK, C], F32, name="gf", align_bytes=64)
+            nc.vector.tensor_tensor(
+                gf[e][:, t, :],
+                dy[t][:].indirect(offs_t[:, e * (C // 16) : (e + 1) * (C // 16)]),
+                gate_t[:, e * C : (e + 1) * C],
+                ALU.mult,
+            )
+
+        def interleave(e):
+            gb[e] = ring2.tile([P, C, PACK], BF16, name="gb", align_bytes=64)
+            nc.scalar.copy(gb[e][:], gf[e][:].rearrange("p t n -> p n t"))
+
+        def quant_g(e):
+            gq[e] = ring2.tile([P, C], U32, name="gq", align_bytes=64)
+            gs[e] = ring2.tile([P, C], U8, name="gs", align_bytes=64)
+            nc.vector.quantize_mx(
+                out=gq[e][:].bitcast(FP8X4), scales=gs[e][:], in_=gb[e][:].rearrange("p n t -> p (n t)")
+            )
+
+        def first(e, b):
+            for h in range(HH):
+                bank = ps1.tile([P, PACK, P], F32, name="bank")
+                banks[e, b, h] = bank
+                for r in range(PACK):
+                    c0 = (h * PACK + r) * P
+                    nc.tensor.matmul_mx(
+                        out=bank[:, r, :],
+                        lhsT=w2_perm[:, e, 2 * c0 : 2 * (c0 + P)].bitcast(FP4X4),
+                        lhsT_scale=w2s[:, e, c0 : c0 + P],
+                        rhs=gq[e][:, b * P : (b + 1) * P].bitcast(FP8X4),
+                        rhs_scale=gs[e][:, b * P : (b + 1) * P],
+                        start=True,
+                        stop=True,
+                    )
+
+        def prep(e):
+            for h in range(HH):
+                sw[e, h] = ring7.tile([P, 2, C, PACK], F32, name="sw", align_bytes=64)
+                nc.scalar.activation(sw[e, h][:, 0], a1_t[e][h][:].rearrange("p r n -> p n r"), ACT.Sigmoid)
+            qs = [a1_t[e][h][:].rearrange("p r n -> p (r n)") for h in range(HH)]
+            for h in range(HH):
+                nc.scalar.activation(qs[h], sw[e, h][:, 0].rearrange("p n r -> p (n r)"), ACT.Square, bias=-0.5)
+            for h in range(HH):
+                nc.scalar.activation(sw[e, h][:, 1].rearrange("p n r -> p (n r)"), qs[h], ACT.Identity, bias=0.25, scale=-1.0)
+
+        def weigh(e, h):
+            for b, engine in ((0, ON0), (1, ON1)):
+                cols = slice(b * P, (b + 1) * P)
+                (nc.vector, nc.gpsimd)[engine].tensor_tensor(
+                    sw[e, h][:, 1, cols], sw[e, h][:, 1, cols], a3_t[e][h][:, :, cols].rearrange("p r n -> p n r"), ALU.mult
+                )
+
+        def da(e, b, h):
+            if h == 0:
+                dt[e, b] = ring2.tile([P, HH, 2, P, PACK], BF16, name="dt", align_bytes=64)
+            nc.vector.tensor_tensor(
+                dt[e, b][:, h],
+                banks[e, b, h][:].rearrange("p r n -> p n r").unsqueeze(1).to_broadcast([P, 2, P, PACK]),
+                sw[e, h][:, :, b * P : (b + 1) * P, :],
+                ALU.mult,
+            )
+
+        dqs, acc = {}, {}
+
+        def quant_d(e, b):
+            dq = ring3.tile([P, HH * 2 * P], U32, name="dq", align_bytes=64)
+            ds = ring3.tile([P, HH * 2 * P], U8, name="ds", align_bytes=64)
+            nc.vector.quantize_mx(
+                out=dq[:].bitcast(FP8X4), scales=ds[:], in_=dt[e, b][:].rearrange("p h j n r -> p (h j n r)")
+            )
+            dqs[e, b] = dq, ds
+
+        def second(e, b):
+            dq, ds = dqs[e, b]
+            acc[e, b] = ps2.tile([P, PACK, P], F32, name="acc")
+            for m in range(KM):
+                for i in range(2 * HH):
+                    h, j = divmod(i, 2)
+                    nc.tensor.matmul_mx(
+                        out=acc[e, b][:, m, :],
+                        lhsT=w13[j][:, e, h, 2 * m * P : 2 * (m + 1) * P].bitcast(FP4X4),
+                        lhsT_scale=w13s[j][:, e, h, m * P : (m + 1) * P],
+                        rhs=dq[:, i * P : (i + 1) * P].bitcast(FP8X4),
+                        rhs_scale=ds[:, i * P : (i + 1) * P],
+                        start=(i == 0),
+                        stop=(i == 2 * HH - 1),
+                    )
+
+        def copy_dx(e, b):
+            s0 = e * C + b * P
+            if (e, b) == (E - 1, B - 1):
+                for m in range(KM):
+                    nc.scalar.copy(dxs[:, m, s0 : s0 + P], acc[e, b][:, m, :])
+            else:
+                nc.scalar.copy(dxs[:, :, s0 : s0 + P], acc[e, b][:, 0:KM, :])
+
+        permute_words(0)
+        for t in range(PACK):
+            gather(0, t)
+        permute_scales(0)
+        interleave(0)
+        prep(0)
+        for t in range(PACK):
+            gather(1, t)
+        quant_g(0)
+        first(0, 0)
+        first(0, 1)
+        interleave(1)
+        prep(1)
+        permute_words(1)
+        for e in range(1, E):
+            permute_scales(e)
+        weigh(0, 0)
+        weigh(0, 1)
+        for e in range(E):
+            more, more2 = e + 1 < E, e + 2 < E
+            if more2:
+                prep(e + 2)
+            da(e, 0, 0)
+            if e:
+                copy_dx(e - 1, 1)
+            if more2:
+                gather(e + 2, 0)
+                gather(e + 2, 1)
+            da(e, 0, 1)
+            if more:
+                quant_g(e + 1)
+                first(e + 1, 0)
+                weigh(e + 1, 0)
+            da(e, 1, 0)
+            quant_d(e, 0)
+            second(e, 0)
+            if more2:
+                gather(e + 2, 2)
+                gather(e + 2, 3)
+                interleave(e + 2)
+            copy_dx(e, 0)
+            da(e, 1, 1)
+            if more:
+                weigh(e + 1, 1)
+                first(e + 1, 1)
+            if more2:
+                permute_words(e + 2)
+            quant_d(e, 1)
+            second(e, 1)
+        copy_dx(E - 1, 1)
+
+        got, res = {}, {}
+
+        def fetch(m, i, lo, hi):
+            lst = (pos1_t, pos2_t)[i]
+            if lo == 0:
+                got[m, i] = ring2.tile([P, T], F32, name=f"got{i}", align_bytes=64)
+            nc.vector.tensor_copy(got[m, i][:, lo:hi], dxs[:, m, :].indirect(lst[:, lo // 16 : hi // 16]))
+
+        def total(m, lo, hi):
+            if lo == 0:
+                res[m] = ring3.tile([P, T], F32, name="res", align_bytes=64)
+            nc.vector.tensor_tensor(res[m][:, lo:hi], got[m, 0][:, lo:hi], got[m, 1][:, lo:hi], ALU.add)
+            nc.sync.dma_start(out[m * P : (m + 1) * P, lo:hi], res[m][:, lo:hi])
+
+        fetch(0, 0, 0, T)
+        fetch(0, 1, 0, T)
+        fetch(1, 0, 0, T)
+        total(0, 0, T)
+        fetch(1, 1, 0, T)
+        fetch(2, 0, 0, T)
+        total(1, 0, T)
+        fetch(2, 1, 0, T // 2)
+        fetch(2, 1, T // 2, T)
+        total(2, 0, T // 2)
+        total(2, T // 2, T)

@@ -8,7 +8,8 @@ PACK = 4
 HH = 2
 B = 2
 KM = K // P
-ON0, ON1 = 0, 0
+NC = HH * B
+AHEAD = 3
 
 F32 = mybir.dt.float32
 BF16 = mybir.dt.bfloat16
@@ -33,7 +34,7 @@ def tile_moe_bdx_glu_sigmoid_kernel(
         keep = ctx.enter_context(tc.tile_pool(name="keep", bufs=1))
         ring2 = ctx.enter_context(tc.tile_pool(name="ring2", bufs=2))
         ring3 = ctx.enter_context(tc.tile_pool(name="ring3", bufs=3))
-        ring7 = ctx.enter_context(tc.tile_pool(name="ring7", bufs=7))
+        ring4 = ctx.enter_context(tc.tile_pool(name="ring4", bufs=4))
         ps1 = ctx.enter_context(tc.psum_pool(name="ps1", bufs=6))
         ps2 = ctx.enter_context(tc.psum_pool(name="ps2", bufs=2))
 
@@ -50,6 +51,7 @@ def tile_moe_bdx_glu_sigmoid_kernel(
         gate_t = keep.tile([P, E * C], F32, name="gate_t", align_bytes=64)
         a1_t = [[keep.tile([P, PACK, C], F32, name=f"a1_{e}_{h}", align_bytes=64) for h in range(HH)] for e in range(E)]
         a3_t = [[keep.tile([P, PACK, C], F32, name=f"a3_{e}_{h}", align_bytes=64) for h in range(HH)] for e in range(E)]
+        fac = keep.tile([P, (AHEAD + 1) * NC, P * PACK], F32, name="fac", align_bytes=64)
         dxs = keep.tile([P, KM, E * C], F32, name="dxs", align_bytes=64)
 
         nc.vector.memset(w2s_raw[:].rearrange("p e i -> p (e i)").bitcast(I32), 0)
@@ -70,17 +72,17 @@ def tile_moe_bdx_glu_sigmoid_kernel(
         def load_gate(lo, hi):
             nc.sync.dma_start(gate_t[:, lo * C : hi * C], gate[0:P, lo * C : hi * C])
 
-        def load_w13(j):
-            words, scales = ((w3_words, w3_scales), (w1_words, w1_scales))[j]
-            for q in range(4):
-                nc.sync.dma_start(
-                    w13s[j][32 * q : 32 * q + 4, :, :, :].rearrange("p e s k -> p (e s) k").bitcast(I32),
-                    scales[:, :, 4 * q : 4 * q + 4, :].rearrange("e s f k -> f (e s) k").bitcast(I32),
-                )
-            nc.sync.dma_start(
-                w13[j][:].rearrange("p e s k -> p (e s) k").bitcast(I32),
-                words.rearrange("e s p k -> p (e s) k").bitcast(I32),
-            )
+        def load_w13s():
+            for j, scales in enumerate((w3_scales, w1_scales)):
+                for q in range(4):
+                    nc.sync.dma_start(
+                        w13s[j][32 * q : 32 * q + 4, :, :, :].rearrange("p e s k -> p (e s) k").bitcast(I32),
+                        scales[:, :, 4 * q : 4 * q + 4, :].rearrange("e s f k -> f (e s) k").bitcast(I32),
+                    )
+
+        def load_w13(e):
+            for j, words in enumerate((w3_words, w1_words)):
+                nc.sync.dma_start(w13[j][:, e].bitcast(I32), words[e].rearrange("s p k -> p s k").bitcast(I32))
 
         def load_w2s():
             for q in range(4):
@@ -91,32 +93,36 @@ def tile_moe_bdx_glu_sigmoid_kernel(
 
         nc.sync.dma_start(offs_t[:], offs)
         load_w2(0)
+        load_a(0, 0, 1)
+        load_w2s()
         load_gate(0, 1)
         for t in range(PACK):
             nc.sync.dma_start(dy[t][:], dy_v[:, t, :])
-        load_a(0, 0, 1)
-        load_gate(1, 2)
-        load_w2s()
         load_a(0, 1, 1)
+        load_gate(1, 2)
         load_w2(1)
         load_a(0, 0, 3)
         load_a(0, 1, 3)
-        load_gate(2, E)
         load_a(1, 0, 1)
         load_a(1, 1, 1)
+        load_w13s()
         load_w13(0)
-        load_w13(1)
+        load_gate(2, E)
         load_a(1, 0, 3)
         load_a(1, 1, 3)
         load_w2(2)
-        for h in range(HH):
-            load_a(2, h, 1)
-        for h in range(HH):
-            load_a(2, h, 3)
+        load_a(2, 0, 1)
+        load_a(2, 1, 1)
+        load_w13(1)
+        load_a(2, 0, 3)
+        load_a(2, 1, 3)
+        load_a(3, 0, 1)
+        load_a(3, 1, 1)
         load_w2(3)
-        for which in (1, 3):
-            for h in range(HH):
-                load_a(3, h, which)
+        load_w13(2)
+        load_a(3, 0, 3)
+        load_a(3, 1, 3)
+        load_w13(3)
         nc.sync.dma_start(pos1_t[:], pos1)
         nc.sync.dma_start(pos2_t[:], pos2)
 
@@ -136,7 +142,7 @@ def tile_moe_bdx_glu_sigmoid_kernel(
 
         def gather(e, t):
             if t == 0:
-                gf[e] = ring2.tile([P, PACK, C], F32, name="gf", align_bytes=64)
+                gf[e] = ring3.tile([P, PACK, C], F32, name="gf", align_bytes=64)
             nc.vector.tensor_tensor(
                 gf[e][:, t, :],
                 dy[t][:].indirect(offs_t[:, e * (C // 16) : (e + 1) * (C // 16)]),
@@ -145,7 +151,7 @@ def tile_moe_bdx_glu_sigmoid_kernel(
             )
 
         def interleave(e):
-            gb[e] = ring2.tile([P, C, PACK], BF16, name="gb", align_bytes=64)
+            gb[e] = ring3.tile([P, C, PACK], BF16, name="gb", align_bytes=64)
             nc.scalar.copy(gb[e][:], gf[e][:].rearrange("p t n -> p n t"))
 
         def quant_g(e):
@@ -171,30 +177,46 @@ def tile_moe_bdx_glu_sigmoid_kernel(
                         stop=True,
                     )
 
-        def prep(e):
-            for h in range(HH):
-                sw[e, h] = ring7.tile([P, 2, C, PACK], F32, name="sw", align_bytes=64)
-                nc.scalar.activation(sw[e, h][:, 0], a1_t[e][h][:].rearrange("p r n -> p n r"), ACT.Sigmoid)
-            qs = [a1_t[e][h][:].rearrange("p r n -> p (r n)") for h in range(HH)]
-            for h in range(HH):
-                nc.scalar.activation(qs[h], sw[e, h][:, 0].rearrange("p n r -> p (n r)"), ACT.Square, bias=-0.5)
-            for h in range(HH):
-                nc.scalar.activation(sw[e, h][:, 1].rearrange("p n r -> p (n r)"), qs[h], ACT.Identity, bias=0.25, scale=-1.0)
+        def s_row(e, h, b):
+            return (e % AHEAD) * NC + h * B + b
 
-        def weigh(e, h):
-            for b, engine in ((0, ON0), (1, ON1)):
-                cols = slice(b * P, (b + 1) * P)
-                (nc.vector, nc.gpsimd)[engine].tensor_tensor(
-                    sw[e, h][:, 1, cols], sw[e, h][:, 1, cols], a3_t[e][h][:, :, cols].rearrange("p r n -> p n r"), ALU.mult
+        def w_row(h, b):
+            return AHEAD * NC + h * B + b
+
+        def prep_a(e, hs):
+            for h in hs:
+                i = s_row(e, h, 0)
+                nc.scalar.activation(
+                    fac[:, i : i + B, :].rearrange("p b (n r) -> p (b n) r", r=PACK),
+                    a1_t[e][h][:].rearrange("p r n -> p n r"),
+                    ACT.Sigmoid,
                 )
 
+        def prep_b(e, hs):
+            ds = [a1_t[e][h][:].rearrange("p r n -> p (r n)") for h in range(HH)]
+            for h in hs:
+                i = s_row(e, h, 0)
+                nc.scalar.activation(ds[h], fac[:, i : i + B, :].rearrange("p b x -> p (b x)"), ACT.Square, bias=-0.5)
+            for h in hs:
+                nc.scalar.activation(ds[h], ds[h], ACT.Identity, bias=0.25, scale=-1.0)
+
+        def weigh(engine, e, h, b):
+            d = a1_t[e][h][:].rearrange("p r n -> p (r n)")[:, b * P * PACK : (b + 1) * P * PACK]
+            engine.tensor_tensor(
+                fac[:, w_row(h, b), :].rearrange("p (n r) -> p n r", r=PACK),
+                d.rearrange("p (n r) -> p n r", r=PACK),
+                a3_t[e][h][:, :, b * P : (b + 1) * P].rearrange("p r n -> p n r"),
+                ALU.mult,
+            )
+
         def da(e, b, h):
-            if h == 0:
-                dt[e, b] = ring2.tile([P, HH, 2, P, PACK], BF16, name="dt", align_bytes=64)
+            if (e, b) not in dt:
+                dt[e, b] = ring3.tile([P, HH, 2, P, PACK], BF16, name="dt", align_bytes=64)
+            s, w = s_row(e, h, b), w_row(h, b)
             nc.vector.tensor_tensor(
                 dt[e, b][:, h],
                 banks[e, b, h][:].rearrange("p r n -> p n r").unsqueeze(1).to_broadcast([P, 2, P, PACK]),
-                sw[e, h][:, :, b * P : (b + 1) * P, :],
+                fac[:, s : w + 1 : w - s, :].rearrange("p j (n r) -> p j n r", r=PACK),
                 ALU.mult,
             )
 
@@ -232,55 +254,63 @@ def tile_moe_bdx_glu_sigmoid_kernel(
             else:
                 nc.scalar.copy(dxs[:, :, s0 : s0 + P], acc[e, b][:, 0:KM, :])
 
+        both = range(HH)
+        prep_a(0, [0])
+        prep_b(0, [0])
         permute_words(0)
+        for e in range(E):
+            permute_scales(e)
         for t in range(PACK):
             gather(0, t)
-        permute_scales(0)
         interleave(0)
-        prep(0)
+        prep_a(0, [1])
+        prep_b(0, [1])
         for t in range(PACK):
             gather(1, t)
         quant_g(0)
         first(0, 0)
         first(0, 1)
+        prep_a(1, both)
+        prep_b(1, both)
         interleave(1)
-        prep(1)
         permute_words(1)
-        for e in range(1, E):
-            permute_scales(e)
-        weigh(0, 0)
-        weigh(0, 1)
         for e in range(E):
             more, more2 = e + 1 < E, e + 2 < E
             if more2:
-                prep(e + 2)
-            da(e, 0, 0)
+                prep_a(e + 2, both)
             if e:
+                copy_dx(e - 1, 0)
                 copy_dx(e - 1, 1)
             if more2:
-                gather(e + 2, 0)
-                gather(e + 2, 1)
-            da(e, 0, 1)
+                prep_b(e + 2, both)
+            for c in range(NC):
+                h, b = divmod(c, B) if more else divmod(c, HH)[::-1]
+                if e == 0 and b == 0:
+                    weigh(nc.vector, 0, h, 0)
+                    weigh(nc.vector, 0, h, 1)
+                da(e, b, h)
+                if more and c < NC - 1:
+                    weigh(nc.gpsimd, e + 1, h, b)
+                if not more and h == HH - 1:
+                    quant_d(e, b)
+                    second(e, b)
+            if more:
+                quant_d(e, 0)
+                second(e, 0)
+            if more2:
+                for t in range(PACK):
+                    gather(e + 2, t)
+                interleave(e + 2)
             if more:
                 quant_g(e + 1)
                 first(e + 1, 0)
-                weigh(e + 1, 0)
-            da(e, 1, 0)
-            quant_d(e, 0)
-            second(e, 0)
-            if more2:
-                gather(e + 2, 2)
-                gather(e + 2, 3)
-                interleave(e + 2)
-            copy_dx(e, 0)
-            da(e, 1, 1)
-            if more:
-                weigh(e + 1, 1)
+                weigh(nc.vector, e + 1, HH - 1, B - 1)
                 first(e + 1, 1)
+                quant_d(e, 1)
+                second(e, 1)
             if more2:
                 permute_words(e + 2)
-            quant_d(e, 1)
-            second(e, 1)
+        copy_dx(E - 1, 0)
         copy_dx(E - 1, 1)
 
         got, res = {}, {}
@@ -294,7 +324,8 @@ def tile_moe_bdx_glu_sigmoid_kernel(
         def total(m, lo, hi):
             if lo == 0:
                 res[m] = ring3.tile([P, T], F32, name="res", align_bytes=64)
-            nc.vector.tensor_tensor(res[m][:, lo:hi], got[m, 0][:, lo:hi], got[m, 1][:, lo:hi], ALU.add)
+            adder = nc.gpsimd if m < KM - 1 else nc.vector
+            adder.tensor_tensor(res[m][:, lo:hi], got[m, 0][:, lo:hi], got[m, 1][:, lo:hi], ALU.add)
             nc.sync.dma_start(out[m * P : (m + 1) * P, lo:hi], res[m][:, lo:hi])
 
         fetch(0, 0, 0, T)

@@ -8,6 +8,7 @@ PACK = 4
 HH = 2
 B = 2
 KM = K // P
+RUN = 4
 NC = HH * B
 AHEAD = 3
 
@@ -51,7 +52,7 @@ def tile_moe_bdx_glu_sigmoid_kernel(
         gate_t = keep.tile([P, E * C], F32, name="gate_t", align_bytes=64)
         a1_t = [[keep.tile([P, PACK, C], F32, name=f"a1_{e}_{h}", align_bytes=64) for h in range(HH)] for e in range(E)]
         a3_t = [[keep.tile([P, PACK, C], F32, name=f"a3_{e}_{h}", align_bytes=64) for h in range(HH)] for e in range(E)]
-        fac = keep.tile([P, (AHEAD + 1) * NC, P * PACK], F32, name="fac", align_bytes=64)
+        fac = keep.tile([P, 2, AHEAD * NC, P * PACK], F32, name="fac", align_bytes=64)
         dxs = keep.tile([P, KM, E * C], F32, name="dxs", align_bytes=64)
 
         nc.vector.memset(w2s_raw[:].rearrange("p e i -> p (e i)").bitcast(I32), 0)
@@ -98,11 +99,11 @@ def tile_moe_bdx_glu_sigmoid_kernel(
         load_gate(0, 1)
         for t in range(PACK):
             nc.sync.dma_start(dy[t][:], dy_v[:, t, :])
-        load_a(0, 1, 1)
-        load_gate(1, 2)
-        load_w2(1)
         load_a(0, 0, 3)
+        load_gate(1, 2)
+        load_a(0, 1, 1)
         load_a(0, 1, 3)
+        load_w2(1)
         load_a(1, 0, 1)
         load_a(1, 1, 1)
         load_w13s()
@@ -152,7 +153,9 @@ def tile_moe_bdx_glu_sigmoid_kernel(
 
         def interleave(e):
             gb[e] = ring3.tile([P, C, PACK], BF16, name="gb", align_bytes=64)
-            nc.scalar.copy(gb[e][:], gf[e][:].rearrange("p t n -> p n t"))
+            nc.scalar.copy(
+                gb[e][:].rearrange("p (n i) t -> p n t i", i=RUN), gf[e][:].rearrange("p t (n i) -> p n t i", i=RUN)
+            )
 
         def quant_g(e):
             gq[e] = ring2.tile([P, C], U32, name="gq", align_bytes=64)
@@ -177,46 +180,45 @@ def tile_moe_bdx_glu_sigmoid_kernel(
                         stop=True,
                     )
 
-        def s_row(e, h, b):
-            return (e % AHEAD) * NC + h * B + b
+        def rows(e, h):
+            i = (e % AHEAD) * NC + h * B
+            return slice(i, i + B)
 
-        def w_row(h, b):
-            return AHEAD * NC + h * B + b
+        def turned(e, h, tile, j, func, scale):
+            nc.scalar.activation(
+                fac[:, j, rows(e, h), :].rearrange("p b (n i r) -> p (b n) r i", i=RUN, r=PACK),
+                tile[e][h][:].rearrange("p r (n i) -> p n r i", i=RUN),
+                func,
+                scale=scale,
+            )
 
-        def prep_a(e, hs):
-            for h in hs:
-                i = s_row(e, h, 0)
-                nc.scalar.activation(
-                    fac[:, i : i + B, :].rearrange("p b (n r) -> p (b n) r", r=PACK),
-                    a1_t[e][h][:].rearrange("p r n -> p n r"),
-                    ACT.Sigmoid,
-                )
+        def prep_s(e, h):
+            turned(e, h, a1_t, 0, ACT.Sigmoid, 1.0)
 
-        def prep_b(e, hs):
-            ds = [a1_t[e][h][:].rearrange("p r n -> p (r n)") for h in range(HH)]
-            for h in hs:
-                i = s_row(e, h, 0)
-                nc.scalar.activation(ds[h], fac[:, i : i + B, :].rearrange("p b x -> p (b x)"), ACT.Square, bias=-0.5)
-            for h in hs:
-                nc.scalar.activation(ds[h], ds[h], ACT.Identity, bias=0.25, scale=-1.0)
+        def prep_q(e, h):
+            nc.scalar.activation(
+                a1_t[e][h][:].rearrange("p r n -> p (r n)"),
+                fac[:, 0, rows(e, h), :].rearrange("p b x -> p (b x)"),
+                ACT.Square,
+                bias=-0.5,
+            )
 
-        def weigh(engine, e, h, b):
-            d = a1_t[e][h][:].rearrange("p r n -> p (r n)")[:, b * P * PACK : (b + 1) * P * PACK]
-            engine.tensor_tensor(
-                fac[:, w_row(h, b), :].rearrange("p (n r) -> p n r", r=PACK),
-                d.rearrange("p (n r) -> p n r", r=PACK),
-                a3_t[e][h][:, :, b * P : (b + 1) * P].rearrange("p r n -> p n r"),
-                ALU.mult,
+        def prep_a(e, h):
+            turned(e, h, a3_t, 1, ACT.Copy, -1.0)
+
+        def weigh(e, h):
+            w = fac[:, 1, rows(e, h), :].rearrange("p b x -> p (b x)")
+            nc.vector.scalar_tensor_tensor(
+                w, a1_t[e][h][:].rearrange("p r n -> p (r n)"), 0.25, w, op0=ALU.subtract, op1=ALU.mult
             )
 
         def da(e, b, h):
             if (e, b) not in dt:
                 dt[e, b] = ring3.tile([P, HH, 2, P, PACK], BF16, name="dt", align_bytes=64)
-            s, w = s_row(e, h, b), w_row(h, b)
             nc.vector.tensor_tensor(
                 dt[e, b][:, h],
                 banks[e, b, h][:].rearrange("p r n -> p n r").unsqueeze(1).to_broadcast([P, 2, P, PACK]),
-                fac[:, s : w + 1 : w - s, :].rearrange("p j (n r) -> p j n r", r=PACK),
+                fac[:, :, rows(e, h).start + b, :].rearrange("p j (n r) -> p j n r", r=PACK),
                 ALU.mult,
             )
 
@@ -254,62 +256,74 @@ def tile_moe_bdx_glu_sigmoid_kernel(
             else:
                 nc.scalar.copy(dxs[:, :, s0 : s0 + P], acc[e, b][:, 0:KM, :])
 
-        both = range(HH)
-        prep_a(0, [0])
-        prep_b(0, [0])
+        prep_s(0, 0)
+        prep_q(0, 0)
         permute_words(0)
         for e in range(E):
             permute_scales(e)
         for t in range(PACK):
             gather(0, t)
+        prep_a(0, 0)
         interleave(0)
-        prep_a(0, [1])
-        prep_b(0, [1])
+        prep_s(0, 1)
+        prep_q(0, 1)
+        prep_a(0, 1)
         for t in range(PACK):
             gather(1, t)
         quant_g(0)
         first(0, 0)
         first(0, 1)
-        prep_a(1, both)
-        prep_b(1, both)
-        interleave(1)
+        weigh(0, 0)
         permute_words(1)
+        for h in range(HH):
+            prep_s(1, h)
+        interleave(1)
+        for h in range(HH):
+            prep_q(1, h)
+        for h in range(HH):
+            prep_a(1, h)
         for e in range(E):
             more, more2 = e + 1 < E, e + 2 < E
             if more2:
-                prep_a(e + 2, both)
+                for h in range(HH):
+                    prep_s(e + 2, h)
             if e:
                 copy_dx(e - 1, 0)
                 copy_dx(e - 1, 1)
             if more2:
-                prep_b(e + 2, both)
+                for h in range(HH):
+                    prep_q(e + 2, h)
+                for h in range(HH):
+                    prep_a(e + 2, h)
             for c in range(NC):
                 h, b = divmod(c, B) if more else divmod(c, HH)[::-1]
-                if e == 0 and b == 0:
-                    weigh(nc.vector, 0, h, 0)
-                    weigh(nc.vector, 0, h, 1)
                 da(e, b, h)
-                if more and c < NC - 1:
-                    weigh(nc.gpsimd, e + 1, h, b)
+                if e == 0 and c == 1:
+                    weigh(0, 1)
                 if not more and h == HH - 1:
                     quant_d(e, b)
                     second(e, b)
+            if more2:
+                gather(e + 2, 0)
+                gather(e + 2, 1)
             if more:
                 quant_d(e, 0)
                 second(e, 0)
             if more2:
-                for t in range(PACK):
-                    gather(e + 2, t)
+                gather(e + 2, 2)
+                gather(e + 2, 3)
                 interleave(e + 2)
             if more:
                 quant_g(e + 1)
                 first(e + 1, 0)
-                weigh(nc.vector, e + 1, HH - 1, B - 1)
+                weigh(e + 1, 0)
                 first(e + 1, 1)
                 quant_d(e, 1)
                 second(e, 1)
             if more2:
                 permute_words(e + 2)
+            if more:
+                weigh(e + 1, 1)
         copy_dx(E - 1, 0)
         copy_dx(E - 1, 1)
 
@@ -324,8 +338,7 @@ def tile_moe_bdx_glu_sigmoid_kernel(
         def total(m, lo, hi):
             if lo == 0:
                 res[m] = ring3.tile([P, T], F32, name="res", align_bytes=64)
-            adder = nc.gpsimd if m < KM - 1 else nc.vector
-            adder.tensor_tensor(res[m][:, lo:hi], got[m, 0][:, lo:hi], got[m, 1][:, lo:hi], ALU.add)
+            (nc.vector if m == KM - 1 else nc.gpsimd).tensor_tensor(res[m][:, lo:hi], got[m, 0][:, lo:hi], got[m, 1][:, lo:hi], ALU.add)
             nc.sync.dma_start(out[m * P : (m + 1) * P, lo:hi], res[m][:, lo:hi])
 
         fetch(0, 0, 0, T)

@@ -76,7 +76,7 @@ def tile_moe_bdx_glu_sigmoid_kernel(
         def load_w13s():
             for j, scales in enumerate((w3_scales, w1_scales)):
                 for q in range(4):
-                    nc.sync.dma_start(
+                    nc.gpsimd.dma_start(
                         w13s[j][32 * q : 32 * q + 4, :, :, :].rearrange("p e s k -> p (e s) k").bitcast(I32),
                         scales[:, :, 4 * q : 4 * q + 4, :].rearrange("e s f k -> f (e s) k").bitcast(I32),
                     )
@@ -87,28 +87,28 @@ def tile_moe_bdx_glu_sigmoid_kernel(
 
         def load_w2s():
             for q in range(4):
-                nc.sync.dma_start(
+                nc.scalar.dma_start(
                     w2s_raw[32 * q : 32 * q + 4, :, :].bitcast(I32),
                     w2_scales[:, 0, 4 * q : 4 * q + 4, :].rearrange("e f i -> f e i").bitcast(I32),
                 )
 
+        load_w2s()
+        load_w13s()
         nc.sync.dma_start(offs_t[:], offs)
         load_w2(0)
-        load_a(0, 0, 1)
-        load_w2s()
         load_gate(0, 1)
         for t in range(PACK):
             nc.sync.dma_start(dy[t][:], dy_v[:, t, :])
-        load_a(0, 0, 3)
         load_gate(1, 2)
+        load_a(0, 0, 1)
+        load_a(0, 0, 3)
         load_a(0, 1, 1)
         load_a(0, 1, 3)
         load_w2(1)
+        load_gate(2, E)
         load_a(1, 0, 1)
         load_a(1, 1, 1)
-        load_w13s()
         load_w13(0)
-        load_gate(2, E)
         load_a(1, 0, 3)
         load_a(1, 1, 3)
         load_w2(2)
@@ -117,9 +117,9 @@ def tile_moe_bdx_glu_sigmoid_kernel(
         load_w13(1)
         load_a(2, 0, 3)
         load_a(2, 1, 3)
+        load_w2(3)
         load_a(3, 0, 1)
         load_a(3, 1, 1)
-        load_w2(3)
         load_w13(2)
         load_a(3, 0, 3)
         load_a(3, 1, 3)
@@ -133,10 +133,10 @@ def tile_moe_bdx_glu_sigmoid_kernel(
                 w2_raw[e][:].bitcast(U16).rearrange("p (h q r) -> p h r q", h=HH, r=PACK),
             )
 
-        def permute_scales(e):
+        def permute_scales(lo, hi):
             nc.vector.tensor_copy(
-                w2s[:, e, :].rearrange("p (h r q) -> p h r q", h=HH, r=PACK),
-                w2s_raw[:, e, :].rearrange("p (h q r) -> p h r q", h=HH, r=PACK),
+                w2s[:, lo:hi, :].rearrange("p e (h r q) -> p (e h) r q", h=HH, r=PACK),
+                w2s_raw[:, lo:hi, :].rearrange("p e (h q r) -> p (e h) r q", h=HH, r=PACK),
             )
 
         gf, gb, gq, gs, sw, banks, dt = {}, {}, {}, {}, {}, {}, {}
@@ -256,23 +256,23 @@ def tile_moe_bdx_glu_sigmoid_kernel(
             else:
                 nc.scalar.copy(dxs[:, :, s0 : s0 + P], acc[e, b][:, 0:KM, :])
 
-        prep_s(0, 0)
-        prep_q(0, 0)
         permute_words(0)
-        for e in range(E):
-            permute_scales(e)
         for t in range(PACK):
             gather(0, t)
-        prep_a(0, 0)
         interleave(0)
+        prep_s(0, 0)
+        prep_q(0, 0)
+        prep_a(0, 0)
         prep_s(0, 1)
         prep_q(0, 1)
         prep_a(0, 1)
         for t in range(PACK):
             gather(1, t)
+        permute_scales(0, 1)
         quant_g(0)
         first(0, 0)
         first(0, 1)
+        permute_scales(1, E)
         weigh(0, 0)
         permute_words(1)
         for h in range(HH):
@@ -297,14 +297,17 @@ def tile_moe_bdx_glu_sigmoid_kernel(
                     prep_a(e + 2, h)
             for c in range(NC):
                 h, b = divmod(c, B) if more else divmod(c, HH)[::-1]
+                if e == 0 and c == B:
+                    gather(2, 0)
                 da(e, b, h)
                 if e == 0 and c == 1:
                     weigh(0, 1)
-                if not more and h == HH - 1:
-                    quant_d(e, b)
-                    second(e, b)
+                if not more and c == NC - 2:
+                    quant_d(e, 0)
+                    second(e, 0)
             if more2:
-                gather(e + 2, 0)
+                if e:
+                    gather(e + 2, 0)
                 gather(e + 2, 1)
             if more:
                 quant_d(e, 0)
@@ -318,8 +321,8 @@ def tile_moe_bdx_glu_sigmoid_kernel(
                 first(e + 1, 0)
                 weigh(e + 1, 0)
                 first(e + 1, 1)
-                quant_d(e, 1)
-                second(e, 1)
+            quant_d(e, 1)
+            second(e, 1)
             if more2:
                 permute_words(e + 2)
             if more:

from contextlib import ExitStack

import concourse.mybir as mybir

N, T, H, K, E, C = 512, 512, 1024, 384, 4, 256
P = 128
PACK = 4
HH = 2
B = 2
KM = K // P
RUN = 4
NC = HH * B
AHEAD = 3

F32 = mybir.dt.float32
BF16 = mybir.dt.bfloat16
U32 = mybir.dt.uint32
I32 = mybir.dt.int32
U16 = mybir.dt.uint16
U8 = mybir.dt.uint8
FP8X4 = mybir.dt.float8_e4m3fn_x4
FP4X4 = mybir.dt.float4_e2m1fn_x4
ACT = mybir.ActivationFunctionType
ALU = mybir.AluOpType

FLOPS = 2 * E * C * H * (N + 2 * K)
BYTES = (N * T + 2 * H * E * C + E * C + K * T) * 4 + E * (N + 2 * K) * H // 2 + E * (N + 2 * K) * H // 32 + 2 * 2 * P * (E * C // 16)


def tile_moe_bdx_glu_sigmoid_kernel(
    tc, dyT, a1, a3, w2_words, w2_scales, w1_words, w1_scales, w3_words, w3_scales, gate, offs, pos1, pos2, out
):
    nc = tc.nc
    with ExitStack() as ctx:
        keep = ctx.enter_context(tc.tile_pool(name="keep", bufs=1))
        ring2 = ctx.enter_context(tc.tile_pool(name="ring2", bufs=2))
        ring3 = ctx.enter_context(tc.tile_pool(name="ring3", bufs=3))
        ring4 = ctx.enter_context(tc.tile_pool(name="ring4", bufs=4))
        ps1 = ctx.enter_context(tc.psum_pool(name="ps1", bufs=6))
        ps2 = ctx.enter_context(tc.psum_pool(name="ps2", bufs=2))

        offs_t = keep.tile([P, E * C // 16], U16, name="offs_t")
        pos1_t = keep.tile([P, T // 16], U16, name="pos1_t")
        pos2_t = keep.tile([P, T // 16], U16, name="pos2_t")
        w2_raw = [ring2.tile([P, 2 * H], U8, name="w2_raw", align_bytes=64) for e in range(E)]
        w2_perm = keep.tile([P, E, 2 * H], U8, name="w2_perm", align_bytes=64)
        w2s_raw = keep.tile([P, E, H], U8, name="w2s_raw", align_bytes=64)
        w2s = keep.tile([P, E, H], U8, name="w2s", align_bytes=64)
        w13 = [keep.tile([P, E, HH, 2 * K], U8, name=f"w13_{j}", align_bytes=64) for j in range(2)]
        w13s = [keep.tile([P, E, HH, K], U8, name=f"w13s_{j}", align_bytes=64) for j in range(2)]
        dy = [keep.tile([P, T], F32, name=f"dy_{t}", align_bytes=64) for t in range(PACK)]
        gate_t = keep.tile([P, E * C], F32, name="gate_t", align_bytes=64)
        a1_t = [[keep.tile([P, PACK, C], F32, name=f"a1_{e}_{h}", align_bytes=64) for h in range(HH)] for e in range(E)]
        a3_t = [[keep.tile([P, PACK, C], F32, name=f"a3_{e}_{h}", align_bytes=64) for h in range(HH)] for e in range(E)]
        fac = keep.tile([P, 2, AHEAD * NC, P * PACK], F32, name="fac", align_bytes=64)
        dxs = keep.tile([P, KM, E * C], F32, name="dxs", align_bytes=64)

        nc.vector.memset(w2s_raw[:].rearrange("p e i -> p (e i)").bitcast(I32), 0)
        for j in range(2):
            nc.gpsimd.memset(w13s[j][:].rearrange("p e s k -> p (e s k)").bitcast(I32), 0)

        a1_v = a1.rearrange("(h q r) c -> h q r c", h=HH, r=PACK)
        a3_v = a3.rearrange("(h q r) c -> h q r c", h=HH, r=PACK)
        dy_v = dyT.rearrange("(q t) c -> q t c", t=PACK)

        def load_w2(e):
            nc.sync.dma_start(w2_raw[e][:].bitcast(I32), w2_words[e, 0].bitcast(I32))

        def load_a(e, h, which):
            tiles, view = (a1_t, a1_v) if which == 1 else (a3_t, a3_v)
            nc.sync.dma_start(tiles[e][h][:], view[h][:, :, e * C : (e + 1) * C])

        def load_gate(lo, hi):
            nc.sync.dma_start(gate_t[:, lo * C : hi * C], gate[0:P, lo * C : hi * C])

        def load_w13s():
            for j, scales in enumerate((w3_scales, w1_scales)):
                for q in range(4):
                    nc.gpsimd.dma_start(
                        w13s[j][32 * q : 32 * q + 4, :, :, :].rearrange("p e s k -> p (e s) k").bitcast(I32),
                        scales[:, :, 4 * q : 4 * q + 4, :].rearrange("e s f k -> f (e s) k").bitcast(I32),
                    )

        def load_w13(e):
            for j, words in enumerate((w3_words, w1_words)):
                nc.sync.dma_start(w13[j][:, e].bitcast(I32), words[e].rearrange("s p k -> p s k").bitcast(I32))

        def load_w2s():
            for q in range(4):
                nc.scalar.dma_start(
                    w2s_raw[32 * q : 32 * q + 4, :, :].bitcast(I32),
                    w2_scales[:, 0, 4 * q : 4 * q + 4, :].rearrange("e f i -> f e i").bitcast(I32),
                )

        load_w2s()
        load_w13s()
        nc.sync.dma_start(offs_t[:], offs)
        load_w2(0)
        load_gate(0, 1)
        for t in range(PACK):
            nc.sync.dma_start(dy[t][:], dy_v[:, t, :])
        load_gate(1, 2)
        load_a(0, 0, 1)
        load_a(0, 0, 3)
        load_a(0, 1, 1)
        load_a(0, 1, 3)
        load_w2(1)
        load_gate(2, E)
        load_a(1, 0, 1)
        load_a(1, 1, 1)
        load_w13(0)
        load_a(1, 0, 3)
        load_a(1, 1, 3)
        load_w2(2)
        load_a(2, 0, 1)
        load_a(2, 1, 1)
        load_w13(1)
        load_a(2, 0, 3)
        load_a(2, 1, 3)
        load_w2(3)
        load_a(3, 0, 1)
        load_a(3, 1, 1)
        load_w13(2)
        load_a(3, 0, 3)
        load_a(3, 1, 3)
        load_w13(3)
        nc.sync.dma_start(pos1_t[:], pos1)
        nc.sync.dma_start(pos2_t[:], pos2)

        def permute_words(e):
            nc.vector.tensor_copy(
                w2_perm[:, e, :].bitcast(U16).rearrange("p (h r q) -> p h r q", h=HH, r=PACK),
                w2_raw[e][:].bitcast(U16).rearrange("p (h q r) -> p h r q", h=HH, r=PACK),
            )

        def permute_scales(lo, hi):
            nc.vector.tensor_copy(
                w2s[:, lo:hi, :].rearrange("p e (h r q) -> p (e h) r q", h=HH, r=PACK),
                w2s_raw[:, lo:hi, :].rearrange("p e (h q r) -> p (e h) r q", h=HH, r=PACK),
            )

        gf, gb, gq, gs, sw, banks, dt = {}, {}, {}, {}, {}, {}, {}

        def gather(e, t):
            if t == 0:
                gf[e] = ring3.tile([P, PACK, C], F32, name="gf", align_bytes=64)
            nc.vector.tensor_tensor(
                gf[e][:, t, :],
                dy[t][:].indirect(offs_t[:, e * (C // 16) : (e + 1) * (C // 16)]),
                gate_t[:, e * C : (e + 1) * C],
                ALU.mult,
            )

        def interleave(e):
            gb[e] = ring3.tile([P, C, PACK], BF16, name="gb", align_bytes=64)
            nc.scalar.copy(
                gb[e][:].rearrange("p (n i) t -> p n t i", i=RUN), gf[e][:].rearrange("p t (n i) -> p n t i", i=RUN)
            )

        def quant_g(e):
            gq[e] = ring2.tile([P, C], U32, name="gq", align_bytes=64)
            gs[e] = ring2.tile([P, C], U8, name="gs", align_bytes=64)
            nc.vector.quantize_mx(
                out=gq[e][:].bitcast(FP8X4), scales=gs[e][:], in_=gb[e][:].rearrange("p n t -> p (n t)")
            )

        def first(e, b):
            for h in range(HH):
                bank = ps1.tile([P, PACK, P], F32, name="bank")
                banks[e, b, h] = bank
                for r in range(PACK):
                    c0 = (h * PACK + r) * P
                    nc.tensor.matmul_mx(
                        out=bank[:, r, :],
                        lhsT=w2_perm[:, e, 2 * c0 : 2 * (c0 + P)].bitcast(FP4X4),
                        lhsT_scale=w2s[:, e, c0 : c0 + P],
                        rhs=gq[e][:, b * P : (b + 1) * P].bitcast(FP8X4),
                        rhs_scale=gs[e][:, b * P : (b + 1) * P],
                        start=True,
                        stop=True,
                    )

        def rows(e, h):
            i = (e % AHEAD) * NC + h * B
            return slice(i, i + B)

        def turned(e, h, tile, j, func, scale):
            nc.scalar.activation(
                fac[:, j, rows(e, h), :].rearrange("p b (n i r) -> p (b n) r i", i=RUN, r=PACK),
                tile[e][h][:].rearrange("p r (n i) -> p n r i", i=RUN),
                func,
                scale=scale,
            )

        def prep_s(e, h):
            turned(e, h, a1_t, 0, ACT.Sigmoid, 1.0)

        def prep_q(e, h):
            nc.scalar.activation(
                a1_t[e][h][:].rearrange("p r n -> p (r n)"),
                fac[:, 0, rows(e, h), :].rearrange("p b x -> p (b x)"),
                ACT.Square,
                bias=-0.5,
            )

        def prep_a(e, h):
            turned(e, h, a3_t, 1, ACT.Copy, -1.0)

        def weigh(e, h):
            w = fac[:, 1, rows(e, h), :].rearrange("p b x -> p (b x)")
            nc.vector.scalar_tensor_tensor(
                w, a1_t[e][h][:].rearrange("p r n -> p (r n)"), 0.25, w, op0=ALU.subtract, op1=ALU.mult
            )

        def da(e, b, h):
            if (e, b) not in dt:
                dt[e, b] = ring3.tile([P, HH, 2, P, PACK], BF16, name="dt", align_bytes=64)
            nc.vector.tensor_tensor(
                dt[e, b][:, h],
                banks[e, b, h][:].rearrange("p r n -> p n r").unsqueeze(1).to_broadcast([P, 2, P, PACK]),
                fac[:, :, rows(e, h).start + b, :].rearrange("p j (n r) -> p j n r", r=PACK),
                ALU.mult,
            )

        dqs, acc = {}, {}

        def quant_d(e, b):
            dq = ring3.tile([P, HH * 2 * P], U32, name="dq", align_bytes=64)
            ds = ring3.tile([P, HH * 2 * P], U8, name="ds", align_bytes=64)
            nc.vector.quantize_mx(
                out=dq[:].bitcast(FP8X4), scales=ds[:], in_=dt[e, b][:].rearrange("p h j n r -> p (h j n r)")
            )
            dqs[e, b] = dq, ds

        def second(e, b):
            dq, ds = dqs[e, b]
            acc[e, b] = ps2.tile([P, PACK, P], F32, name="acc")
            for m in range(KM):
                for i in range(2 * HH):
                    h, j = divmod(i, 2)
                    nc.tensor.matmul_mx(
                        out=acc[e, b][:, m, :],
                        lhsT=w13[j][:, e, h, 2 * m * P : 2 * (m + 1) * P].bitcast(FP4X4),
                        lhsT_scale=w13s[j][:, e, h, m * P : (m + 1) * P],
                        rhs=dq[:, i * P : (i + 1) * P].bitcast(FP8X4),
                        rhs_scale=ds[:, i * P : (i + 1) * P],
                        start=(i == 0),
                        stop=(i == 2 * HH - 1),
                    )

        def copy_dx(e, b):
            s0 = e * C + b * P
            if (e, b) == (E - 1, B - 1):
                for m in range(KM):
                    nc.scalar.copy(dxs[:, m, s0 : s0 + P], acc[e, b][:, m, :])
            else:
                nc.scalar.copy(dxs[:, :, s0 : s0 + P], acc[e, b][:, 0:KM, :])

        permute_words(0)
        for t in range(PACK):
            gather(0, t)
        interleave(0)
        prep_s(0, 0)
        prep_q(0, 0)
        prep_a(0, 0)
        prep_s(0, 1)
        prep_q(0, 1)
        prep_a(0, 1)
        for t in range(PACK):
            gather(1, t)
        permute_scales(0, 1)
        quant_g(0)
        first(0, 0)
        first(0, 1)
        permute_scales(1, E)
        weigh(0, 0)
        permute_words(1)
        for h in range(HH):
            prep_s(1, h)
        interleave(1)
        for h in range(HH):
            prep_q(1, h)
        for h in range(HH):
            prep_a(1, h)
        for e in range(E):
            more, more2 = e + 1 < E, e + 2 < E
            if more2:
                for h in range(HH):
                    prep_s(e + 2, h)
            if e:
                copy_dx(e - 1, 0)
                copy_dx(e - 1, 1)
            if more2:
                for h in range(HH):
                    prep_q(e + 2, h)
                for h in range(HH):
                    prep_a(e + 2, h)
            for c in range(NC):
                h, b = divmod(c, B) if more else divmod(c, HH)[::-1]
                if e == 0 and c == B:
                    gather(2, 0)
                da(e, b, h)
                if e == 0 and c == 1:
                    weigh(0, 1)
                if not more and c == NC - 2:
                    quant_d(e, 0)
                    second(e, 0)
            if more2:
                if e:
                    gather(e + 2, 0)
                gather(e + 2, 1)
            if more:
                quant_d(e, 0)
                second(e, 0)
            if more2:
                gather(e + 2, 2)
                gather(e + 2, 3)
                interleave(e + 2)
            if more:
                quant_g(e + 1)
                first(e + 1, 0)
                weigh(e + 1, 0)
                first(e + 1, 1)
            quant_d(e, 1)
            second(e, 1)
            if more2:
                permute_words(e + 2)
            if more:
                weigh(e + 1, 1)
        copy_dx(E - 1, 0)
        copy_dx(E - 1, 1)

        got, res = {}, {}

        def fetch(m, i, lo, hi):
            lst = (pos1_t, pos2_t)[i]
            if lo == 0:
                got[m, i] = ring2.tile([P, T], F32, name=f"got{i}", align_bytes=64)
            nc.vector.tensor_copy(got[m, i][:, lo:hi], dxs[:, m, :].indirect(lst[:, lo // 16 : hi // 16]))

        def total(m, lo, hi):
            if lo == 0:
                res[m] = ring3.tile([P, T], F32, name="res", align_bytes=64)
            (nc.vector if m == KM - 1 else nc.gpsimd).tensor_tensor(res[m][:, lo:hi], got[m, 0][:, lo:hi], got[m, 1][:, lo:hi], ALU.add)
            nc.sync.dma_start(out[m * P : (m + 1) * P, lo:hi], res[m][:, lo:hi])

        fetch(0, 0, 0, T)
        fetch(0, 1, 0, T)
        fetch(1, 0, 0, T)
        total(0, 0, T)
        fetch(1, 1, 0, T)
        fetch(2, 0, 0, T)
        total(1, 0, T)
        fetch(2, 1, 0, T // 2)
        fetch(2, 1, T // 2, T)
        total(2, 0, T // 2)
        total(2, T // 2, T)
